import numpy as np
import ml_dtypes


def mxq(x, axis, fmt="e4m3"):
    dtype, down = {"e4m3": (ml_dtypes.float8_e4m3fn, 7), "e5m2": (ml_dtypes.float8_e5m2, 14)}[fmt]
    v = np.moveaxis(np.asarray(x, np.float32).astype(ml_dtypes.bfloat16).astype(np.float64), axis, -1)
    blocks = v.reshape(v.shape[:-1] + (-1, 32))
    amax = np.abs(blocks).max(-1, keepdims=True)
    byte = np.maximum(np.where(amax > 0, np.frexp(amax)[1] - 1 + 127, 0) - down, 1)
    scale = np.exp2(byte - 127.0)
    codes = (blocks / scale).astype(np.float32).astype(dtype).astype(np.float64)
    return np.moveaxis((codes * scale).reshape(v.shape), -1, axis)


WIDE = False


def mx_kscale(k):
    if not WIDE:
        return np.ones(k)
    levels = np.array([10, -10, 5, -5, 0])
    if k % 512:
        return np.exp2(np.random.permutation(np.resize(levels, k // 32))).repeat(32)
    a = np.empty((k // 512, 16))
    for p in range(k // 512):
        a[p, :8] = np.random.permutation(np.resize(levels, 8))
        for g in range(8):
            far = levels[np.abs(levels - a[p, g]) >= 10]
            a[p, g + 8] = far[np.random.randint(len(far))]
    return np.exp2(a.ravel()).repeat(32)


def f64(x):
    return np.asarray(x).astype(np.float64)


def striped(idx):
    return np.tile(np.asarray(idx).reshape(-1, 16).T, (8, 1)).astype(np.uint16)


def unstriped(offs):
    return offs[:16].T.reshape(-1).astype(np.int64)


E2M1 = np.array([0.0, 0.5, 1.0, 1.5, 2.0, 3.0, 4.0, 6.0, -0.0, -0.5, -1.0, -1.5, -2.0, -3.0, -4.0, -6.0])


def pack_weight(w, fmt):
    k, n = w.shape
    w = f64(np.asarray(w, np.float32).astype(ml_dtypes.bfloat16)).reshape(k // 32, 32, n)
    amax = np.abs(w).max(1)
    if fmt == "e4m3":
        byte = np.frexp(amax)[1] - 1 + 127 - 7
    else:
        mant, ex = np.frexp(amax / 6.0)
        byte = np.where(mant > 0.5, ex, ex - 1) + 127
    byte = np.clip(np.where(amax > 0, byte, 1), 1, 254)
    scaled = (w * np.exp2(127.0 - byte)[:, None, :]).reshape(k, n).astype(np.float32)
    by_word = np.ascontiguousarray(scaled.reshape(k // 512, 128, 4, n).transpose(0, 1, 3, 2))
    if fmt == "e4m3":
        words = by_word.astype(ml_dtypes.float8_e4m3fn).view(np.uint8)
    else:
        c = by_word.astype(ml_dtypes.float4_e2m1fn).view(np.uint8) & 0xF
        words = (c[..., 0::2] | (c[..., 1::2] << 4)).reshape(k // 512, 128, 2 * n)
    return np.ascontiguousarray(words), np.ascontiguousarray(byte.astype(np.uint8).reshape(k // 512, 16, n))


def unpack_weight(words, scales, fmt):
    g, _, n = scales.shape
    words = np.ascontiguousarray(words).reshape(g, 128, n, -1)
    if fmt == "e4m3":
        vals = words.view(ml_dtypes.float8_e4m3fn).astype(np.float64)
    else:
        nib = np.empty((g, 128, n, 4), np.uint8)
        nib[..., 0::2] = words & 0xF
        nib[..., 1::2] = words >> 4
        vals = E2M1[nib]
    vals = vals * np.repeat(np.exp2(scales.astype(np.float64) - 127.0), 8, axis=1)[..., None]
    return vals.transpose(0, 1, 3, 2).reshape(g * 512, n)


def bf(x):
    return np.asarray(x, np.float32).astype(ml_dtypes.bfloat16)


def planes(Y):
    r, m = Y.shape
    b = f64(bf(Y)).reshape(r // 32, 32, m)
    amax = np.abs(b).max(1)
    byte = np.clip(np.where(amax > 0, np.frexp(amax)[1] - 1 + 127 - 7, 1), 1, 254)
    codes = (b * np.exp2(127.0 - byte)[:, None, :]).reshape(r, m).astype(np.float32).astype(ml_dtypes.float8_e4m3fn).view(np.uint8)
    words = codes.reshape(r // 512, 128, 4, m).transpose(0, 1, 3, 2)
    return np.ascontiguousarray(words), np.ascontiguousarray(byte.astype(np.uint8).reshape(r // 512, 16, m))


D, T, I, Q, E, U = 512, 2048, 512, 256, 512, 256


def setup_inputs():
    n = np.random.standard_normal
    idx = np.random.permutation(T)[:I]
    idx2 = np.repeat(np.random.permutation(U)[:I // 16], 16)
    fd = mx_kscale(D)
    fi = mx_kscale(I)
    ti = np.ones(T)
    ti[idx] = fi
    keysp = pack_weight(n((D, T)) / fd[:, None], "e2m1")
    return {
        "query": (n((D, Q)) * 0.4 / np.sqrt(D) * fd[:, None]).astype(np.float32),
        "keys_words": keysp[0],
        "keys_scales": keysp[1],
        "kscale": np.tile(np.random.uniform(0.4, 2.0, U), (128, 1)).astype(np.float32),
        "vscale": np.tile(np.random.uniform(0.4, 2.0, U), (128, 1)).astype(np.float32),
        "size": (np.random.uniform(0.5, 2.0, (1, I)) * fi).astype(np.float32),
        "vals": (n((E, T)) / ti).astype(np.float32),
        "offs": striped(idx),
        "offs2": striped(idx2),
    }


def reference(query, keys_words, keys_scales, kscale, vscale, size, vals, offs, offs2):
    idx = unstriped(offs)
    idx2 = unstriped(offs2)
    keysu = unpack_weight(keys_words, keys_scales, "e2m1")
    queryq = mxq(f64(query), 0, "e4m3")
    keysidxg = keysu[:, idx]
    a = queryq.T @ keysidxg
    s = a * f64(kscale)[:1][:, idx2]
    p = np.exp(s - np.max(s, axis=1, keepdims=True))
    w = p * f64(vscale)[:1][:, idx2] * f64(size) / np.sum(p, axis=1, keepdims=True)
    wt = w.T
    vt = f64(vals)[:, idx].T
    vtq = mxq(vt, 0, "e4m3")
    wtq = mxq(wt, 0, "e4m3")
    o = vtq.T @ wtq
    words, scales = planes(o)
    return o, words, scales

@@ -1,0 +1,200 @@
+from contextlib import ExitStack
+
+import concourse.mybir as mybir
+from concourse.masks import make_identity
+
+D, T, I, Q, E, U = 512, 2048, 512, 256, 512, 256
+FLOPS = 2 * D * I * Q + 2 * I * E * Q
+
+F32 = mybir.dt.float32
+BF16 = mybir.dt.bfloat16
+I32 = mybir.dt.int32
+U32 = mybir.dt.uint32
+U16 = mybir.dt.uint16
+U8 = mybir.dt.uint8
+FP8X4 = mybir.dt.float8_e4m3fn_x4
+FP4X4 = mybir.dt.float4_e2m1fn_x4
+ACT = mybir.ActivationFunctionType
+ALU = mybir.AluOpType
+
+P = 128
+PACK = 4
+HALVES = Q // P
+KS_WINDOW = 704
+VS_WINDOW = 544
+PAGE_ROWS = 32
+
+
+def tile_attend_pagescales_pl_kernel(tc, query, keys_words, keys_scales, kscale, vscale, size, vals, offs, offs2, out_0, out_1, out_2):
+    nc = tc.nc
+    with ExitStack() as ctx:
+        sb = ctx.enter_context(tc.tile_pool(name="sb", bufs=1))
+        ps = ctx.enter_context(tc.psum_pool(name="ps", bufs=1))
+
+        def bank(number, shape, name):
+            return ps.tile(shape, F32, name=name, tag="bank%d" % number)
+
+        tokens = sb.tile([P, I // 16], U16, name="tokens")
+        pages = sb.tile([P, I // 16], U16, name="pages")
+        ks_win = sb.tile([P, KS_WINDOW], F32, name="ks_win")
+        vs_win = sb.tile([P, VS_WINDOW], F32, name="vs_win")
+        size_col = sb.tile([P, PACK], F32, name="size_col")
+        kw_win = sb.tile([P, T], U16, name="kw_win", align_bytes=64)
+        kb_win = sb.tile([P, T], U8, name="kb_win", align_bytes=64)
+        q_raw = sb.tile([P, PACK, Q], F32, name="q_raw", tag="q_raw", align_bytes=64)
+        v_win = [sb.tile([P, T], F32, name="v_win%d" % j, tag="v_win%d" % j, align_bytes=64) for j in range(PACK)]
+        ident = sb.tile([P, P], F32, name="ident")
+        warm_in = sb.tile([P, 1], F32, name="warm_in")
+        warm_out = sb.tile([P, 1], F32, name="warm_out")
+
+        nc.gpsimd.memset(kb_win[:].bitcast(I32), 0)
+        nc.vector.memset(ks_win[:, U:], 0.0)
+        nc.vector.memset(ks_win[32:64, :U], 0.0)
+        nc.vector.memset(ks_win[64:, :U], 0.0)
+        nc.vector.memset(vs_win[:, U:], 0.0)
+        nc.vector.memset(warm_in[:], 0.0)
+        nc.scalar.activation(out=warm_out[:], in_=warm_in[:], func=ACT.Exp)
+        make_identity(nc, ident[:])
+
+        nc.sync.dma_start(pages[:], offs2)
+        nc.sync.dma_start(ks_win[:PAGE_ROWS, :U], kscale[:PAGE_ROWS, :])
+        nc.sync.dma_start(size_col[:], size[0].rearrange("(p t) -> p t", t=PACK))
+        nc.sync.dma_start(tokens[:], offs)
+        nc.sync.dma_start(kw_win[:].bitcast(I32), keys_words[0].bitcast(I32))
+        nc.sync.dma_start(q_raw[:], query.rearrange("(p t) q -> p t q", t=PACK))
+        for quad in range(4):
+            nc.sync.dma_start(kb_win[32 * quad : 32 * quad + 4, :].bitcast(I32), keys_scales[0, 4 * quad : 4 * quad + 4, :].bitcast(I32))
+        nc.sync.dma_start(vs_win[:, :U], vscale)
+        v_rows = vals.rearrange("(p j) t -> p j t", j=PACK)
+        for j in range(PACK):
+            nc.sync.dma_start(v_win[j][:], v_rows[:, j, :])
+
+        ks_row = sb.tile([P, I], F32, name="ks_row")
+        nc.vector.tensor_copy(ks_row[:], ks_win[:].indirect(pages[:]))
+        ks_t = bank(0, [P, PACK, P], "ks_t")
+        for j in range(PACK):
+            nc.tensor.transpose(ks_t[:, j, :], ks_row[:, j * P : (j + 1) * P], ident[:])
+        ks_col = sb.tile([P, PACK], F32, name="ks_col")
+        nc.scalar.copy(out=ks_col[:], in_=ks_t[:, :, 0])
+
+        size_t = bank(1, [P, PACK, P], "size_t")
+        for t in range(PACK):
+            nc.tensor.transpose(size_t[:, t, :], size_col[:, t : t + 1].to_broadcast([P, P]), ident[:])
+        size_row = sb.tile([P, I], F32, name="size_row")
+        nc.scalar.copy(out=size_row[:].rearrange("p (s t) -> p s t", t=PACK), in_=size_t[:].rearrange("p t s -> p s t"))
+
+        k_words = sb.tile([P, I], U16, name="k_words", align_bytes=64)
+        k_bytes = sb.tile([P, I], U8, name="k_bytes", align_bytes=64)
+        nc.vector.tensor_copy(k_words[:], kw_win[:].indirect(tokens[:]))
+        nc.vector.tensor_copy(k_bytes[:], kb_win[:].indirect(tokens[:]))
+
+        q_bf = sb.tile([P, Q, PACK], BF16, name="q_bf", align_bytes=64)
+        nc.scalar.copy(out=q_bf[:], in_=q_raw[:].rearrange("p t q -> p q t"))
+        q_words = sb.tile([P, Q], U32, name="q_words", align_bytes=64)
+        q_bytes = sb.tile([P, Q], U8, name="q_bytes", align_bytes=64)
+        nc.vector.quantize_mx(out=q_words[:].bitcast(FP8X4), scales=q_bytes[:], in_=q_bf[:].rearrange("p q t -> p (q t)"))
+
+        a_t = [bank(3 + b, [P, 2, Q], "a_t%d" % b) for b in range(2)]
+        s_t = [sb.tile([P, Q], F32, name="s_t%d" % j) for j in range(PACK)]
+        for j in range(PACK):
+            cols = slice(j * P, (j + 1) * P)
+            nc.tensor.matmul_mx(out=a_t[j // 2][:, j % 2, :], lhsT=k_words[:, cols].bitcast(FP4X4), lhsT_scale=k_bytes[:, cols],
+                                rhs=q_words[:].bitcast(FP8X4), rhs_scale=q_bytes[:], start=True, stop=True)
+        for j in range(PACK):
+            nc.scalar.activation(out=s_t[j][:], in_=a_t[j // 2][:, j % 2, :], func=ACT.Copy, scale=ks_col[:, j : j + 1])
+        s = [bank(5 + h, [P, I], "s%d" % h) for h in range(HALVES)]
+        for h in range(HALVES):
+            for j in range(PACK):
+                nc.tensor.transpose(s[h][:, j * P : (j + 1) * P], s_t[j][:, h * P : (h + 1) * P], ident[:])
+
+        f_row = sb.tile([P, I], F32, name="f_row", tag="q_raw", align_bytes=64)
+        nc.vector.tensor_tensor(f_row[:], vs_win[:].indirect(pages[:]), size_row[:], ALU.mult)
+
+        v_words = {j: sb.tile([P, P], U32, name="v_words%d" % j, align_bytes=64) for j in (0, 1, 3)}
+        v_bytes = [sb.tile([P, P], U8, name="v_bytes%d" % j, align_bytes=64) for j in range(PACK)]
+        v_pairs = [sb.tile([P, P, 2], F32, name="v_pairs%d" % j, align_bytes=64) for j in range(PACK)]
+
+        def turn(rows, turned, pairs):
+            words = rows[:].bitcast(F32)
+            for u in range(2):
+                nc.tensor.transpose(turned[:, u, :], words[:, u : I // 2 : 2], ident[:])
+            nc.scalar.copy(out=pairs[:], in_=turned[:].rearrange("p u c -> p c u"))
+
+        def gather_values(j):
+            v_bf = sb.tile([P, I], BF16, name="v_bf%d" % j, align_bytes=64)
+            nc.vector.tensor_copy(v_bf[:], v_win[j][:].indirect(tokens[:]))
+            turn(v_bf, bank((0, 7)[j % 2], [P, 2, P], "v_t%d" % j), v_pairs[j])
+
+        def quantize(pairs, words, scale_bytes):
+            nc.vector.quantize_mx(out=words.bitcast(FP8X4), scales=scale_bytes, in_=pairs[:].rearrange("p c u -> p (c u)").bitcast(BF16))
+
+        gather_values(0)
+
+        neg_max = [sb.tile([P, 1], F32, name="neg_max0", tag="v_win0", align_bytes=64), sb.tile([P, 1], F32, name="neg_max1")]
+        total = [sb.tile([P, 1], F32, name="total%d" % h) for h in range(HALVES)]
+        p = [sb.tile([P, I], F32, name="p%d" % h) for h in range(HALVES)]
+        for h in range(HALVES):
+            nc.vector.tensor_reduce(out=neg_max[h][:], in_=s[h][:], axis=mybir.AxisListType.X, op=ALU.max, negate=True)
+            nc.scalar.activation(out=p[h][:], in_=s[h][:], func=ACT.Exp, bias=neg_max[h][:], accum_out=total[h][:])
+
+        gather_values(1)
+        quantize(v_pairs[0], v_words[0][:], v_bytes[0][:])
+
+        inv = [sb.tile([P, 1], F32, name="inv0", tag="v_win1", align_bytes=64), sb.tile([P, 1], F32, name="inv1")]
+        w_bytes = sb.tile([P, Q], U8, name="w_bytes", align_bytes=64)
+        w_pairs = [sb.tile([P, P, 2], F32, name="w_pairs%d" % h, align_bytes=64) for h in range(HALVES)]
+        for h in range(HALVES):
+            nc.vector.reciprocal(out=inv[h][:], in_=total[h][:])
+        for h in range(HALVES):
+            w_bf = sb.tile([P, I], BF16, name="w_bf%d" % h, align_bytes=64)
+            nc.vector.scalar_tensor_tensor(out=w_bf[:], in0=p[h][:], scalar=inv[h][:], in1=f_row[:], op0=ALU.mult, op1=ALU.mult)
+            turn(w_bf, bank(5 + h, [P, 2, P], "w_t%d" % h), w_pairs[h])
+
+        gather_values(2)
+        w_words = sb.tile([P, Q], U32, name="w_words", tag="v_win2", align_bytes=64)
+        for h in range(HALVES):
+            cols = slice(h * P, (h + 1) * P)
+            quantize(w_pairs[h], w_words[:, cols], w_bytes[:, cols])
+        quantize(v_pairs[1], v_words[1][:], v_bytes[1][:])
+        gather_values(3)
+        v_words[2] = sb.tile([P, P], U32, name="v_words2", tag="v_win3", align_bytes=64)
+        quantize(v_pairs[2], v_words[2][:], v_bytes[2][:])
+        quantize(v_pairs[3], v_words[3][:], v_bytes[3][:])
+
+        o = [[bank((3, 1)[g] + h, [P, 2, P], "o%d%d" % (g, h)) for h in range(HALVES)] for g in range(2)]
+        o_sb = [sb.tile([P, 2, Q], F32, name="o_sb%d" % g) for g in range(2)]
+        o_bf = [sb.tile([P, P, PACK], BF16, name="o_bf%d" % h, align_bytes=64) for h in range(HALVES)]
+        o_words = sb.tile([P, Q], U32, name="o_words", align_bytes=64)
+        o_bytes = sb.tile([P, Q], U8, name="o_bytes", align_bytes=64)
+        out_rows = out_0.rearrange("(p j) q -> p j q", j=PACK)
+
+        def products(g):
+            for j in (2 * g, 2 * g + 1):
+                for h in range(HALVES):
+                    cols = slice(h * P, (h + 1) * P)
+                    nc.tensor.matmul_mx(out=o[g][h][:, j % 2, :], lhsT=v_words[j][:].bitcast(FP8X4), lhsT_scale=v_bytes[j][:],
+                                        rhs=w_words[:, cols].bitcast(FP8X4), rhs_scale=w_bytes[:, cols], start=True, stop=True)
+
+        def rounded(g, h):
+            return dict(out=o_bf[h][:, :, 2 * g : 2 * g + 2], in_=o[g][h][:].rearrange("p j q -> p q j"))
+
+        def store(g, engine):
+            for h in range(HALVES):
+                nc.scalar.copy(out=o_sb[g][:, :, h * P : (h + 1) * P], in_=o[g][h][:])
+            engine.dma_start(out_rows[:, 2 * g : 2 * g + 2, :], o_sb[g][:])
+
+        products(0)
+        store(0, nc.sync)
+        for h in range(HALVES):
+            nc.scalar.copy(**rounded(0, h))
+        products(1)
+        nc.vector.tensor_copy(**rounded(1, 0))
+        nc.scalar.copy(**rounded(1, 1))
+        for h in range(HALVES):
+            cols = slice(h * P, (h + 1) * P)
+            nc.vector.quantize_mx(out=o_words[:, cols].bitcast(FP8X4), scales=o_bytes[:, cols], in_=o_bf[h][:].rearrange("p q j -> p (q j)"))
+        store(1, nc.scalar)
+        nc.sync.dma_start(out_1[0].rearrange("p c r -> p (c r)").bitcast(I32), o_words[:].bitcast(I32))
+        for quad in range(4):
+            engine = nc.sync if quad < 2 else nc.scalar
+            engine.dma_start(out_2[0, 4 * quad : 4 * quad + 4, :].bitcast(I32), o_bytes[32 * quad : 32 * quad + 4, :].bitcast(I32))

@@ -29,6 +29,8 @@ def tile_attend_pagescales_pl_kernel(tc, query, keys_words, keys_scales, kscale,
     nc = tc.nc
     with ExitStack() as ctx:
         sb = ctx.enter_context(tc.tile_pool(name="sb", bufs=1))
+        last = ctx.enter_context(tc.tile_pool(name="last", bufs=1))
+        second = ctx.enter_context(tc.tile_pool(name="second", bufs=1))
         ps = ctx.enter_context(tc.psum_pool(name="ps", bufs=1))
 
         def bank(number, shape, name):
@@ -40,9 +42,14 @@ def tile_attend_pagescales_pl_kernel(tc, query, keys_words, keys_scales, kscale,
         vs_win = sb.tile([P, VS_WINDOW], F32, name="vs_win")
         size_col = sb.tile([P, PACK], F32, name="size_col")
         kw_win = sb.tile([P, T], U16, name="kw_win", align_bytes=64)
-        kb_win = sb.tile([P, T], U8, name="kb_win", align_bytes=64)
+        kb_win = sb.tile([P, T], U8, name="kb_win", tag="kb_win", align_bytes=64)
         q_raw = sb.tile([P, PACK, Q], F32, name="q_raw", tag="q_raw", align_bytes=64)
-        v_win = [sb.tile([P, T], F32, name="v_win%d" % j, tag="v_win%d" % j, align_bytes=64) for j in range(PACK)]
+        v_win = [
+            sb.tile([P, T], F32, name="v_win0", tag="v_win0", align_bytes=64),
+            second.tile([P, T], F32, name="v_win1", offset=0, align_bytes=64),
+            sb.tile([P, T], F32, name="v_win2", tag="v_win2", align_bytes=64),
+            last.tile([P, T], F32, name="v_win3", offset=0, align_bytes=64),
+        ]
         ident = sb.tile([P, P], F32, name="ident")
         warm_in = sb.tile([P, 1], F32, name="warm_in")
         warm_out = sb.tile([P, 1], F32, name="warm_out")
@@ -58,7 +65,7 @@ def tile_attend_pagescales_pl_kernel(tc, query, keys_words, keys_scales, kscale,
 
         nc.sync.dma_start(pages[:], offs2)
         nc.sync.dma_start(ks_win[:PAGE_ROWS, :U], kscale[:PAGE_ROWS, :])
-        nc.sync.dma_start(size_col[:], size[0].rearrange("(p t) -> p t", t=PACK))
+        nc.scalar.dma_start(size_col[:], size[0].rearrange("(p t) -> p t", t=PACK))
         nc.sync.dma_start(tokens[:], offs)
         nc.sync.dma_start(kw_win[:].bitcast(I32), keys_words[0].bitcast(I32))
         nc.sync.dma_start(q_raw[:], query.rearrange("(p t) q -> p t q", t=PACK))
@@ -69,6 +76,12 @@ def tile_attend_pagescales_pl_kernel(tc, query, keys_words, keys_scales, kscale,
         for j in range(PACK):
             nc.sync.dma_start(v_win[j][:], v_rows[:, j, :])
 
+        size_t = bank(1, [P, PACK, P], "size_t")
+        for t in range(PACK):
+            nc.tensor.transpose(size_t[:, t, :], size_col[:, t : t + 1].to_broadcast([P, P]), ident[:])
+        size_row = sb.tile([P, I], F32, name="size_row")
+        nc.scalar.copy(out=size_row[:].rearrange("p (s t) -> p s t", t=PACK), in_=size_t[:].rearrange("p t s -> p s t"))
+
         ks_row = sb.tile([P, I], F32, name="ks_row")
         nc.vector.tensor_copy(ks_row[:], ks_win[:].indirect(pages[:]))
         ks_t = bank(0, [P, PACK, P], "ks_t")
@@ -77,12 +90,6 @@ def tile_attend_pagescales_pl_kernel(tc, query, keys_words, keys_scales, kscale,
         ks_col = sb.tile([P, PACK], F32, name="ks_col")
         nc.scalar.copy(out=ks_col[:], in_=ks_t[:, :, 0])
 
-        size_t = bank(1, [P, PACK, P], "size_t")
-        for t in range(PACK):
-            nc.tensor.transpose(size_t[:, t, :], size_col[:, t : t + 1].to_broadcast([P, P]), ident[:])
-        size_row = sb.tile([P, I], F32, name="size_row")
-        nc.scalar.copy(out=size_row[:].rearrange("p (s t) -> p s t", t=PACK), in_=size_t[:].rearrange("p t s -> p s t"))
-
         k_words = sb.tile([P, I], U16, name="k_words", align_bytes=64)
         k_bytes = sb.tile([P, I], U8, name="k_bytes", align_bytes=64)
         nc.vector.tensor_copy(k_words[:], kw_win[:].indirect(tokens[:]))
@@ -90,7 +97,7 @@ def tile_attend_pagescales_pl_kernel(tc, query, keys_words, keys_scales, kscale,
 
         q_bf = sb.tile([P, Q, PACK], BF16, name="q_bf", align_bytes=64)
         nc.scalar.copy(out=q_bf[:], in_=q_raw[:].rearrange("p t q -> p q t"))
-        q_words = sb.tile([P, Q], U32, name="q_words", align_bytes=64)
+        q_words = sb.tile([P, Q], U32, name="q_words", tag="kb_win", align_bytes=64)
         q_bytes = sb.tile([P, Q], U8, name="q_bytes", align_bytes=64)
         nc.vector.quantize_mx(out=q_words[:].bitcast(FP8X4), scales=q_bytes[:], in_=q_bf[:].rearrange("p q t -> p (q t)"))
 
@@ -110,9 +117,9 @@ def tile_attend_pagescales_pl_kernel(tc, query, keys_words, keys_scales, kscale,
         f_row = sb.tile([P, I], F32, name="f_row", tag="q_raw", align_bytes=64)
         nc.vector.tensor_tensor(f_row[:], vs_win[:].indirect(pages[:]), size_row[:], ALU.mult)
 
-        v_words = {j: sb.tile([P, P], U32, name="v_words%d" % j, align_bytes=64) for j in (0, 1, 3)}
         v_bytes = [sb.tile([P, P], U8, name="v_bytes%d" % j, align_bytes=64) for j in range(PACK)]
         v_pairs = [sb.tile([P, P, 2], F32, name="v_pairs%d" % j, align_bytes=64) for j in range(PACK)]
+        v_words = []
 
         def turn(rows, turned, pairs):
             words = rows[:].bitcast(F32)
@@ -120,80 +127,90 @@ def tile_attend_pagescales_pl_kernel(tc, query, keys_words, keys_scales, kscale,
                 nc.tensor.transpose(turned[:, u, :], words[:, u : I // 2 : 2], ident[:])
             nc.scalar.copy(out=pairs[:], in_=turned[:].rearrange("p u c -> p c u"))
 
-        def gather_values(j):
-            v_bf = sb.tile([P, I], BF16, name="v_bf%d" % j, align_bytes=64)
+        def gather_values(j, slot):
+            v_bf = sb.tile([P, I], BF16, name="v_bf%d" % j, tag=slot, align_bytes=64)
             nc.vector.tensor_copy(v_bf[:], v_win[j][:].indirect(tokens[:]))
-            turn(v_bf, bank((0, 7)[j % 2], [P, 2, P], "v_t%d" % j), v_pairs[j])
+            return v_bf
+
+        def turn_values(j, v_bf):
+            turn(v_bf, bank((5, 7, 0, 7)[j], [P, 2, P], "v_t%d" % j), v_pairs[j])
 
         def quantize(pairs, words, scale_bytes):
             nc.vector.quantize_mx(out=words.bitcast(FP8X4), scales=scale_bytes, in_=pairs[:].rearrange("p c u -> p (c u)").bitcast(BF16))
 
-        gather_values(0)
+        def quantize_values(j, words):
+            v_words.append(words)
+            quantize(v_pairs[j], v_words[j][:], v_bytes[j][:])
 
-        neg_max = [sb.tile([P, 1], F32, name="neg_max0", tag="v_win0", align_bytes=64), sb.tile([P, 1], F32, name="neg_max1")]
+        v_first = gather_values(0, "v_bf0")
+
+        neg_max = [sb.tile([P, 1], F32, name="neg_max%d" % h, tag=("v_win0", "neg_max1")[h], align_bytes=64) for h in range(HALVES)]
         total = [sb.tile([P, 1], F32, name="total%d" % h) for h in range(HALVES)]
-        p = [sb.tile([P, I], F32, name="p%d" % h) for h in range(HALVES)]
+        p = [sb.tile([P, I], F32, name="p%d" % h, tag="p%d" % h, align_bytes=64) for h in range(HALVES)]
         for h in range(HALVES):
             nc.vector.tensor_reduce(out=neg_max[h][:], in_=s[h][:], axis=mybir.AxisListType.X, op=ALU.max, negate=True)
             nc.scalar.activation(out=p[h][:], in_=s[h][:], func=ACT.Exp, bias=neg_max[h][:], accum_out=total[h][:])
 
-        gather_values(1)
-        quantize(v_pairs[0], v_words[0][:], v_bytes[0][:])
+        turn_values(0, v_first)
+        turn_values(1, gather_values(1, "v_bf1"))
 
-        inv = [sb.tile([P, 1], F32, name="inv0", tag="v_win1", align_bytes=64), sb.tile([P, 1], F32, name="inv1")]
+        inv = [second.tile([P, 1], F32, name="inv%d" % h, offset=64 * h, align_bytes=64) for h in range(HALVES)]
         w_bytes = sb.tile([P, Q], U8, name="w_bytes", align_bytes=64)
-        w_pairs = [sb.tile([P, P, 2], F32, name="w_pairs%d" % h, align_bytes=64) for h in range(HALVES)]
+        w_pairs = [sb.tile([P, P, 2], F32, name="w_pairs%d" % h, tag="w_pairs%d" % h, align_bytes=64) for h in range(HALVES)]
         for h in range(HALVES):
             nc.vector.reciprocal(out=inv[h][:], in_=total[h][:])
         for h in range(HALVES):
             w_bf = sb.tile([P, I], BF16, name="w_bf%d" % h, align_bytes=64)
             nc.vector.scalar_tensor_tensor(out=w_bf[:], in0=p[h][:], scalar=inv[h][:], in1=f_row[:], op0=ALU.mult, op1=ALU.mult)
             turn(w_bf, bank(5 + h, [P, 2, P], "w_t%d" % h), w_pairs[h])
+        quantize_values(0, sb.tile([P, P], U32, name="v_words0", tag="p0", align_bytes=64))
+        quantize_values(1, second.tile([P, P], U32, name="v_words1", offset=64, align_bytes=64))
 
-        gather_values(2)
+        turn_values(2, gather_values(2, "p1"))
         w_words = sb.tile([P, Q], U32, name="w_words", tag="v_win2", align_bytes=64)
         for h in range(HALVES):
             cols = slice(h * P, (h + 1) * P)
             quantize(w_pairs[h], w_words[:, cols], w_bytes[:, cols])
-        quantize(v_pairs[1], v_words[1][:], v_bytes[1][:])
-        gather_values(3)
-        v_words[2] = sb.tile([P, P], U32, name="v_words2", tag="v_win3", align_bytes=64)
-        quantize(v_pairs[2], v_words[2][:], v_bytes[2][:])
-        quantize(v_pairs[3], v_words[3][:], v_bytes[3][:])
+        v_last = gather_values(3, "w_pairs0")
 
         o = [[bank((3, 1)[g] + h, [P, 2, P], "o%d%d" % (g, h)) for h in range(HALVES)] for g in range(2)]
-        o_sb = [sb.tile([P, 2, Q], F32, name="o_sb%d" % g) for g in range(2)]
-        o_bf = [sb.tile([P, P, PACK], BF16, name="o_bf%d" % h, align_bytes=64) for h in range(HALVES)]
+        o_bf = [last.tile([P, P, PACK], BF16, name="o_bf%d" % h, offset=1024 * (h + 1), align_bytes=64) for h in range(HALVES)]
         o_words = sb.tile([P, Q], U32, name="o_words", align_bytes=64)
         o_bytes = sb.tile([P, Q], U8, name="o_bytes", align_bytes=64)
         out_rows = out_0.rearrange("(p j) q -> p j q", j=PACK)
 
-        def products(g):
-            for j in (2 * g, 2 * g + 1):
-                for h in range(HALVES):
-                    cols = slice(h * P, (h + 1) * P)
-                    nc.tensor.matmul_mx(out=o[g][h][:, j % 2, :], lhsT=v_words[j][:].bitcast(FP8X4), lhsT_scale=v_bytes[j][:],
-                                        rhs=w_words[:, cols].bitcast(FP8X4), rhs_scale=w_bytes[:, cols], start=True, stop=True)
+        def product(j):
+            for h in range(HALVES):
+                cols = slice(h * P, (h + 1) * P)
+                nc.tensor.matmul_mx(out=o[j // 2][h][:, j % 2, :], lhsT=v_words[j][:].bitcast(FP8X4), lhsT_scale=v_bytes[j][:],
+                                    rhs=w_words[:, cols].bitcast(FP8X4), rhs_scale=w_bytes[:, cols], start=True, stop=True)
 
         def rounded(g, h):
             return dict(out=o_bf[h][:, :, 2 * g : 2 * g + 2], in_=o[g][h][:].rearrange("p j q -> p q j"))
 
-        def store(g, engine):
+        def store(first, count, engine):
+            o_sb = sb.tile([P, count, Q], F32, name="o_sb%d" % first)
             for h in range(HALVES):
-                nc.scalar.copy(out=o_sb[g][:, :, h * P : (h + 1) * P], in_=o[g][h][:])
-            engine.dma_start(out_rows[:, 2 * g : 2 * g + 2, :], o_sb[g][:])
+                nc.scalar.copy(out=o_sb[:, :, h * P : (h + 1) * P], in_=o[first // 2][h][:, first % 2 : first % 2 + count, :])
+            engine.dma_start(out_rows[:, first : first + count, :], o_sb[:])
 
-        products(0)
-        store(0, nc.sync)
+        quantize_values(2, last.tile([P, P], U32, name="v_words2", offset=0, align_bytes=64))
+        product(0)
+        product(1)
+        store(0, 2, nc.sync)
+        turn_values(3, v_last)
+        product(2)
+        store(2, 1, nc.sync)
         for h in range(HALVES):
-            nc.scalar.copy(**rounded(0, h))
-        products(1)
+            nc.vector.tensor_copy(**rounded(0, h))
+        quantize_values(3, sb.tile([P, P], U32, name="v_words3", align_bytes=64))
+        product(3)
         nc.vector.tensor_copy(**rounded(1, 0))
         nc.scalar.copy(**rounded(1, 1))
-        for h in range(HALVES):
+        for h in reversed(range(HALVES)):
             cols = slice(h * P, (h + 1) * P)
             nc.vector.quantize_mx(out=o_words[:, cols].bitcast(FP8X4), scales=o_bytes[:, cols], in_=o_bf[h][:].rearrange("p q j -> p (q j)"))
-        store(1, nc.scalar)
+        store(3, 1, nc.scalar)
         nc.sync.dma_start(out_1[0].rearrange("p c r -> p (c r)").bitcast(I32), o_words[:].bitcast(I32))
         for quad in range(4):
             engine = nc.sync if quad < 2 else nc.scalar

@@ -31,6 +31,7 @@ def tile_attend_pagescales_pl_kernel(tc, query, keys_words, keys_scales, kscale,
         sb = ctx.enter_context(tc.tile_pool(name="sb", bufs=1))
         last = ctx.enter_context(tc.tile_pool(name="last", bufs=1))
         second = ctx.enter_context(tc.tile_pool(name="second", bufs=1))
+        first = ctx.enter_context(tc.tile_pool(name="first", bufs=1))
         ps = ctx.enter_context(tc.psum_pool(name="ps", bufs=1))
 
         def bank(number, shape, name):
@@ -43,9 +44,9 @@ def tile_attend_pagescales_pl_kernel(tc, query, keys_words, keys_scales, kscale,
         size_col = sb.tile([P, PACK], F32, name="size_col")
         kw_win = sb.tile([P, T], U16, name="kw_win", align_bytes=64)
         kb_win = sb.tile([P, T], U8, name="kb_win", tag="kb_win", align_bytes=64)
-        q_raw = sb.tile([P, PACK, Q], F32, name="q_raw", tag="q_raw", align_bytes=64)
+        q_raw = sb.tile([P, PACK, Q], F32, name="q_raw", tag="q_raw")
         v_win = [
-            sb.tile([P, T], F32, name="v_win0", tag="v_win0", align_bytes=64),
+            first.tile([P, T], F32, name="v_win0", offset=0, align_bytes=64),
             second.tile([P, T], F32, name="v_win1", offset=0, align_bytes=64),
             sb.tile([P, T], F32, name="v_win2", tag="v_win2", align_bytes=64),
             last.tile([P, T], F32, name="v_win3", offset=0, align_bytes=64),
@@ -79,8 +80,6 @@ def tile_attend_pagescales_pl_kernel(tc, query, keys_words, keys_scales, kscale,
         size_t = bank(1, [P, PACK, P], "size_t")
         for t in range(PACK):
             nc.tensor.transpose(size_t[:, t, :], size_col[:, t : t + 1].to_broadcast([P, P]), ident[:])
-        size_row = sb.tile([P, I], F32, name="size_row")
-        nc.scalar.copy(out=size_row[:].rearrange("p (s t) -> p s t", t=PACK), in_=size_t[:].rearrange("p t s -> p s t"))
 
         ks_row = sb.tile([P, I], F32, name="ks_row")
         nc.vector.tensor_copy(ks_row[:], ks_win[:].indirect(pages[:]))
@@ -95,8 +94,10 @@ def tile_attend_pagescales_pl_kernel(tc, query, keys_words, keys_scales, kscale,
         nc.vector.tensor_copy(k_words[:], kw_win[:].indirect(tokens[:]))
         nc.vector.tensor_copy(k_bytes[:], kb_win[:].indirect(tokens[:]))
 
-        q_bf = sb.tile([P, Q, PACK], BF16, name="q_bf", align_bytes=64)
-        nc.scalar.copy(out=q_bf[:], in_=q_raw[:].rearrange("p t q -> p q t"))
+        q_bf = sb.tile([P, Q, PACK], BF16, name="q_bf", tag="q_bf", align_bytes=64)
+        nc.scalar.copy(out=q_bf[:].rearrange("p (c i) t -> p c t i", i=4), in_=q_raw[:].rearrange("p t (c i) -> p c t i", i=4))
+        size_row = sb.tile([P, I], F32, name="size_row", tag="q_raw")
+        nc.scalar.copy(out=size_row[:].rearrange("p (s t) -> p s t", t=PACK), in_=size_t[:].rearrange("p t s -> p s t"))
         q_words = sb.tile([P, Q], U32, name="q_words", tag="kb_win", align_bytes=64)
         q_bytes = sb.tile([P, Q], U8, name="q_bytes", align_bytes=64)
         nc.vector.quantize_mx(out=q_words[:].bitcast(FP8X4), scales=q_bytes[:], in_=q_bf[:].rearrange("p q t -> p (q t)"))
@@ -114,18 +115,18 @@ def tile_attend_pagescales_pl_kernel(tc, query, keys_words, keys_scales, kscale,
             for j in range(PACK):
                 nc.tensor.transpose(s[h][:, j * P : (j + 1) * P], s_t[j][:, h * P : (h + 1) * P], ident[:])
 
-        f_row = sb.tile([P, I], F32, name="f_row", tag="q_raw", align_bytes=64)
+        f_row = sb.tile([P, I], F32, name="f_row", tag="q_bf", align_bytes=64)
         nc.vector.tensor_tensor(f_row[:], vs_win[:].indirect(pages[:]), size_row[:], ALU.mult)
 
-        v_bytes = [sb.tile([P, P], U8, name="v_bytes%d" % j, align_bytes=64) for j in range(PACK)]
-        v_pairs = [sb.tile([P, P, 2], F32, name="v_pairs%d" % j, align_bytes=64) for j in range(PACK)]
+        v_bytes = sb.tile([P, PACK * P], U8, name="v_bytes", align_bytes=64)
+        v_pairs = sb.tile([P, PACK * P, 2], F32, name="v_pairs", align_bytes=64)
         v_words = []
 
         def turn(rows, turned, pairs):
             words = rows[:].bitcast(F32)
             for u in range(2):
                 nc.tensor.transpose(turned[:, u, :], words[:, u : I // 2 : 2], ident[:])
-            nc.scalar.copy(out=pairs[:], in_=turned[:].rearrange("p u c -> p c u"))
+            nc.scalar.copy(out=pairs, in_=turned[:].rearrange("p u c -> p c u"))
 
         def gather_values(j, slot):
             v_bf = sb.tile([P, I], BF16, name="v_bf%d" % j, tag=slot, align_bytes=64)
@@ -133,18 +134,19 @@ def tile_attend_pagescales_pl_kernel(tc, query, keys_words, keys_scales, kscale,
             return v_bf
 
         def turn_values(j, v_bf):
-            turn(v_bf, bank((5, 7, 0, 7)[j], [P, 2, P], "v_t%d" % j), v_pairs[j])
+            turn(v_bf, bank((5, 7, 0, 7)[j], [P, 2, P], "v_t%d" % j), v_pairs[:, j * P : (j + 1) * P, :])
 
         def quantize(pairs, words, scale_bytes):
-            nc.vector.quantize_mx(out=words.bitcast(FP8X4), scales=scale_bytes, in_=pairs[:].rearrange("p c u -> p (c u)").bitcast(BF16))
+            nc.vector.quantize_mx(out=words.bitcast(FP8X4), scales=scale_bytes, in_=pairs.rearrange("p c u -> p (c u)").bitcast(BF16))
 
-        def quantize_values(j, words):
-            v_words.append(words)
-            quantize(v_pairs[j], v_words[j][:], v_bytes[j][:])
+        def quantize_values(start, count, words):
+            cols = slice(start * P, (start + count) * P)
+            quantize(v_pairs[:, cols, :], words[:], v_bytes[:, cols])
+            v_words.extend([words[:, n * P : (n + 1) * P] for n in range(count)])
 
         v_first = gather_values(0, "v_bf0")
 
-        neg_max = [sb.tile([P, 1], F32, name="neg_max%d" % h, tag=("v_win0", "neg_max1")[h], align_bytes=64) for h in range(HALVES)]
+        neg_max = [first.tile([P, 1], F32, name="neg_max%d" % h, offset=64 * h, align_bytes=64) for h in range(HALVES)]
         total = [sb.tile([P, 1], F32, name="total%d" % h) for h in range(HALVES)]
         p = [sb.tile([P, I], F32, name="p%d" % h, tag="p%d" % h, align_bytes=64) for h in range(HALVES)]
         for h in range(HALVES):
@@ -162,15 +164,14 @@ def tile_attend_pagescales_pl_kernel(tc, query, keys_words, keys_scales, kscale,
         for h in range(HALVES):
             w_bf = sb.tile([P, I], BF16, name="w_bf%d" % h, align_bytes=64)
             nc.vector.scalar_tensor_tensor(out=w_bf[:], in0=p[h][:], scalar=inv[h][:], in1=f_row[:], op0=ALU.mult, op1=ALU.mult)
-            turn(w_bf, bank(5 + h, [P, 2, P], "w_t%d" % h), w_pairs[h])
-        quantize_values(0, sb.tile([P, P], U32, name="v_words0", tag="p0", align_bytes=64))
-        quantize_values(1, second.tile([P, P], U32, name="v_words1", offset=64, align_bytes=64))
+            turn(w_bf, bank(5 + h, [P, 2, P], "w_t%d" % h), w_pairs[h][:])
+        quantize_values(0, 2, sb.tile([P, 2 * P], U32, name="v_words01", tag="p0", align_bytes=64))
 
         turn_values(2, gather_values(2, "p1"))
         w_words = sb.tile([P, Q], U32, name="w_words", tag="v_win2", align_bytes=64)
         for h in range(HALVES):
             cols = slice(h * P, (h + 1) * P)
-            quantize(w_pairs[h], w_words[:, cols], w_bytes[:, cols])
+            quantize(w_pairs[h][:], w_words[:, cols], w_bytes[:, cols])
         v_last = gather_values(3, "w_pairs0")
 
         o = [[bank((3, 1)[g] + h, [P, 2, P], "o%d%d" % (g, h)) for h in range(HALVES)] for g in range(2)]
@@ -182,19 +183,19 @@ def tile_attend_pagescales_pl_kernel(tc, query, keys_words, keys_scales, kscale,
         def product(j):
             for h in range(HALVES):
                 cols = slice(h * P, (h + 1) * P)
-                nc.tensor.matmul_mx(out=o[j // 2][h][:, j % 2, :], lhsT=v_words[j][:].bitcast(FP8X4), lhsT_scale=v_bytes[j][:],
+                nc.tensor.matmul_mx(out=o[j // 2][h][:, j % 2, :], lhsT=v_words[j].bitcast(FP8X4), lhsT_scale=v_bytes[:, j * P : (j + 1) * P],
                                     rhs=w_words[:, cols].bitcast(FP8X4), rhs_scale=w_bytes[:, cols], start=True, stop=True)
 
         def rounded(g, h):
             return dict(out=o_bf[h][:, :, 2 * g : 2 * g + 2], in_=o[g][h][:].rearrange("p j q -> p q j"))
 
-        def store(first, count, engine):
-            o_sb = sb.tile([P, count, Q], F32, name="o_sb%d" % first)
+        def store(start, count, engine):
+            o_sb = sb.tile([P, count, Q], F32, name="o_sb%d" % start)
             for h in range(HALVES):
-                nc.scalar.copy(out=o_sb[:, :, h * P : (h + 1) * P], in_=o[first // 2][h][:, first % 2 : first % 2 + count, :])
-            engine.dma_start(out_rows[:, first : first + count, :], o_sb[:])
+                nc.scalar.copy(out=o_sb[:, :, h * P : (h + 1) * P], in_=o[start // 2][h][:, start % 2 : start % 2 + count, :])
+            engine.dma_start(out_rows[:, start : start + count, :], o_sb[:])
 
-        quantize_values(2, last.tile([P, P], U32, name="v_words2", offset=0, align_bytes=64))
+        quantize_values(2, 1, last.tile([P, P], U32, name="v_words2", offset=0, align_bytes=64))
         product(0)
         product(1)
         store(0, 2, nc.sync)
@@ -203,7 +204,7 @@ def tile_attend_pagescales_pl_kernel(tc, query, keys_words, keys_scales, kscale,
         store(2, 1, nc.sync)
         for h in range(HALVES):
             nc.vector.tensor_copy(**rounded(0, h))
-        quantize_values(3, sb.tile([P, P], U32, name="v_words3", align_bytes=64))
+        quantize_values(3, 1, sb.tile([P, P], U32, name="v_words3", align_bytes=64))
         product(3)
         nc.vector.tensor_copy(**rounded(1, 0))
         nc.scalar.copy(**rounded(1, 1))

@@ -66,7 +66,7 @@ def tile_attend_pagescales_pl_kernel(tc, query, keys_words, keys_scales, kscale,
 
         nc.sync.dma_start(pages[:], offs2)
         nc.sync.dma_start(ks_win[:PAGE_ROWS, :U], kscale[:PAGE_ROWS, :])
-        nc.scalar.dma_start(size_col[:], size[0].rearrange("(p t) -> p t", t=PACK))
+        nc.sync.dma_start(size_col[:], size[0].rearrange("(p t) -> p t", t=PACK))
         nc.sync.dma_start(tokens[:], offs)
         nc.sync.dma_start(kw_win[:].bitcast(I32), keys_words[0].bitcast(I32))
         nc.sync.dma_start(q_raw[:], query.rearrange("(p t) q -> p t q", t=PACK))
@@ -77,10 +77,6 @@ def tile_attend_pagescales_pl_kernel(tc, query, keys_words, keys_scales, kscale,
         for j in range(PACK):
             nc.sync.dma_start(v_win[j][:], v_rows[:, j, :])
 
-        size_t = bank(1, [P, PACK, P], "size_t")
-        for t in range(PACK):
-            nc.tensor.transpose(size_t[:, t, :], size_col[:, t : t + 1].to_broadcast([P, P]), ident[:])
-
         ks_row = sb.tile([P, I], F32, name="ks_row")
         nc.vector.tensor_copy(ks_row[:], ks_win[:].indirect(pages[:]))
         ks_t = bank(0, [P, PACK, P], "ks_t")
@@ -89,12 +85,16 @@ def tile_attend_pagescales_pl_kernel(tc, query, keys_words, keys_scales, kscale,
         ks_col = sb.tile([P, PACK], F32, name="ks_col")
         nc.scalar.copy(out=ks_col[:], in_=ks_t[:, :, 0])
 
+        size_t = bank(1, [P, PACK, P], "size_t")
+        for t in range(PACK):
+            nc.tensor.transpose(size_t[:, t, :], size_col[:, t : t + 1].to_broadcast([P, P]), ident[:])
+
         k_words = sb.tile([P, I], U16, name="k_words", align_bytes=64)
         k_bytes = sb.tile([P, I], U8, name="k_bytes", align_bytes=64)
         nc.vector.tensor_copy(k_words[:], kw_win[:].indirect(tokens[:]))
         nc.vector.tensor_copy(k_bytes[:], kb_win[:].indirect(tokens[:]))
 
-        q_bf = sb.tile([P, Q, PACK], BF16, name="q_bf", tag="q_bf", align_bytes=64)
+        q_bf = sb.tile([P, Q, PACK], BF16, name="q_bf", align_bytes=64)
         nc.scalar.copy(out=q_bf[:].rearrange("p (c i) t -> p c t i", i=4), in_=q_raw[:].rearrange("p t (c i) -> p c t i", i=4))
         size_row = sb.tile([P, I], F32, name="size_row", tag="q_raw")
         nc.scalar.copy(out=size_row[:].rearrange("p (s t) -> p s t", t=PACK), in_=size_t[:].rearrange("p t s -> p s t"))
@@ -115,7 +115,7 @@ def tile_attend_pagescales_pl_kernel(tc, query, keys_words, keys_scales, kscale,
             for j in range(PACK):
                 nc.tensor.transpose(s[h][:, j * P : (j + 1) * P], s_t[j][:, h * P : (h + 1) * P], ident[:])
 
-        f_row = sb.tile([P, I], F32, name="f_row", tag="q_bf", align_bytes=64)
+        f_row = sb.tile([P, I], F32, name="f_row")
         nc.vector.tensor_tensor(f_row[:], vs_win[:].indirect(pages[:]), size_row[:], ALU.mult)
 
         v_bytes = sb.tile([P, PACK * P], U8, name="v_bytes", align_bytes=64)

@@ -52,16 +52,12 @@ def tile_attend_pagescales_pl_kernel(tc, query, keys_words, keys_scales, kscale,
             last.tile([P, T], F32, name="v_win3", offset=0, align_bytes=64),
         ]
         ident = sb.tile([P, P], F32, name="ident")
-        warm_in = sb.tile([P, 1], F32, name="warm_in")
-        warm_out = sb.tile([P, 1], F32, name="warm_out")
 
         nc.gpsimd.memset(kb_win[:].bitcast(I32), 0)
         nc.vector.memset(ks_win[:, U:], 0.0)
         nc.vector.memset(ks_win[32:64, :U], 0.0)
         nc.vector.memset(ks_win[64:, :U], 0.0)
         nc.vector.memset(vs_win[:, U:], 0.0)
-        nc.vector.memset(warm_in[:], 0.0)
-        nc.scalar.activation(out=warm_out[:], in_=warm_in[:], func=ACT.Exp)
         make_identity(nc, ident[:])
 
         nc.sync.dma_start(pages[:], offs2)
@@ -181,7 +177,7 @@ def tile_attend_pagescales_pl_kernel(tc, query, keys_words, keys_scales, kscale,
         out_rows = out_0.rearrange("(p j) q -> p j q", j=PACK)
 
         def product(j):
-            for h in range(HALVES):
+            for h in reversed(range(HALVES)):
                 cols = slice(h * P, (h + 1) * P)
                 nc.tensor.matmul_mx(out=o[j // 2][h][:, j % 2, :], lhsT=v_words[j].bitcast(FP8X4), lhsT_scale=v_bytes[:, j * P : (j + 1) * P],
                                     rhs=w_words[:, cols].bitcast(FP8X4), rhs_scale=w_bytes[:, cols], start=True, stop=True)
@@ -191,7 +187,7 @@ def tile_attend_pagescales_pl_kernel(tc, query, keys_words, keys_scales, kscale,
 
         def store(start, count, engine):
             o_sb = sb.tile([P, count, Q], F32, name="o_sb%d" % start)
-            for h in range(HALVES):
+            for h in reversed(range(HALVES)):
                 nc.scalar.copy(out=o_sb[:, :, h * P : (h + 1) * P], in_=o[start // 2][h][:, start % 2 : start % 2 + count, :])
             engine.dma_start(out_rows[:, start : start + count, :], o_sb[:])
 

from contextlib import ExitStack

import concourse.mybir as mybir
from concourse.masks import make_identity

D, T, I, Q, E, U = 512, 2048, 512, 256, 512, 256
FLOPS = 2 * D * I * Q + 2 * I * E * Q

F32 = mybir.dt.float32
BF16 = mybir.dt.bfloat16
I32 = mybir.dt.int32
U32 = mybir.dt.uint32
U16 = mybir.dt.uint16
U8 = mybir.dt.uint8
FP8X4 = mybir.dt.float8_e4m3fn_x4
FP4X4 = mybir.dt.float4_e2m1fn_x4
ACT = mybir.ActivationFunctionType
ALU = mybir.AluOpType

P = 128
PACK = 4
HALVES = Q // P
KS_WINDOW = 704
VS_WINDOW = 544
PAGE_ROWS = 32


def tile_attend_pagescales_pl_kernel(tc, query, keys_words, keys_scales, kscale, vscale, size, vals, offs, offs2, out_0, out_1, out_2):
    nc = tc.nc
    with ExitStack() as ctx:
        sb = ctx.enter_context(tc.tile_pool(name="sb", bufs=1))
        last = ctx.enter_context(tc.tile_pool(name="last", bufs=1))
        second = ctx.enter_context(tc.tile_pool(name="second", bufs=1))
        first = ctx.enter_context(tc.tile_pool(name="first", bufs=1))
        ps = ctx.enter_context(tc.psum_pool(name="ps", bufs=1))

        def bank(number, shape, name):
            return ps.tile(shape, F32, name=name, tag="bank%d" % number)

        tokens = sb.tile([P, I // 16], U16, name="tokens")
        pages = sb.tile([P, I // 16], U16, name="pages")
        ks_win = sb.tile([P, KS_WINDOW], F32, name="ks_win")
        vs_win = sb.tile([P, VS_WINDOW], F32, name="vs_win")
        size_col = sb.tile([P, PACK], F32, name="size_col")
        kw_win = sb.tile([P, T], U16, name="kw_win", align_bytes=64)
        kb_win = sb.tile([P, T], U8, name="kb_win", tag="kb_win", align_bytes=64)
        q_raw = sb.tile([P, PACK, Q], F32, name="q_raw", tag="q_raw")
        v_win = [
            first.tile([P, T], F32, name="v_win0", offset=0, align_bytes=64),
            second.tile([P, T], F32, name="v_win1", offset=0, align_bytes=64),
            sb.tile([P, T], F32, name="v_win2", tag="v_win2", align_bytes=64),
            last.tile([P, T], F32, name="v_win3", offset=0, align_bytes=64),
        ]
        ident = sb.tile([P, P], F32, name="ident")

        nc.gpsimd.memset(kb_win[:].bitcast(I32), 0)
        nc.vector.memset(ks_win[:, U:], 0.0)
        nc.vector.memset(ks_win[32:64, :U], 0.0)
        nc.vector.memset(ks_win[64:, :U], 0.0)
        nc.vector.memset(vs_win[:, U:], 0.0)
        make_identity(nc, ident[:])

        nc.sync.dma_start(pages[:], offs2)
        nc.sync.dma_start(ks_win[:PAGE_ROWS, :U], kscale[:PAGE_ROWS, :])
        nc.sync.dma_start(size_col[:], size[0].rearrange("(p t) -> p t", t=PACK))
        nc.sync.dma_start(tokens[:], offs)
        nc.sync.dma_start(kw_win[:].bitcast(I32), keys_words[0].bitcast(I32))
        nc.sync.dma_start(q_raw[:], query.rearrange("(p t) q -> p t q", t=PACK))
        for quad in range(4):
            nc.sync.dma_start(kb_win[32 * quad : 32 * quad + 4, :].bitcast(I32), keys_scales[0, 4 * quad : 4 * quad + 4, :].bitcast(I32))
        nc.sync.dma_start(vs_win[:, :U], vscale)
        v_rows = vals.rearrange("(p j) t -> p j t", j=PACK)
        for j in range(PACK):
            nc.sync.dma_start(v_win[j][:], v_rows[:, j, :])

        ks_row = sb.tile([P, I], F32, name="ks_row")
        nc.vector.tensor_copy(ks_row[:], ks_win[:].indirect(pages[:]))
        ks_t = bank(0, [P, PACK, P], "ks_t")
        for j in range(PACK):
            nc.tensor.transpose(ks_t[:, j, :], ks_row[:, j * P : (j + 1) * P], ident[:])
        ks_col = sb.tile([P, PACK], F32, name="ks_col")
        nc.scalar.copy(out=ks_col[:], in_=ks_t[:, :, 0])

        size_t = bank(1, [P, PACK, P], "size_t")
        for t in range(PACK):
            nc.tensor.transpose(size_t[:, t, :], size_col[:, t : t + 1].to_broadcast([P, P]), ident[:])

        k_words = sb.tile([P, I], U16, name="k_words", align_bytes=64)
        k_bytes = sb.tile([P, I], U8, name="k_bytes", align_bytes=64)
        nc.vector.tensor_copy(k_words[:], kw_win[:].indirect(tokens[:]))
        nc.vector.tensor_copy(k_bytes[:], kb_win[:].indirect(tokens[:]))

        q_bf = sb.tile([P, Q, PACK], BF16, name="q_bf", align_bytes=64)
        nc.scalar.copy(out=q_bf[:].rearrange("p (c i) t -> p c t i", i=4), in_=q_raw[:].rearrange("p t (c i) -> p c t i", i=4))
        size_row = sb.tile([P, I], F32, name="size_row", tag="q_raw")
        nc.scalar.copy(out=size_row[:].rearrange("p (s t) -> p s t", t=PACK), in_=size_t[:].rearrange("p t s -> p s t"))
        q_words = sb.tile([P, Q], U32, name="q_words", tag="kb_win", align_bytes=64)
        q_bytes = sb.tile([P, Q], U8, name="q_bytes", align_bytes=64)
        nc.vector.quantize_mx(out=q_words[:].bitcast(FP8X4), scales=q_bytes[:], in_=q_bf[:].rearrange("p q t -> p (q t)"))

        a_t = [bank(3 + b, [P, 2, Q], "a_t%d" % b) for b in range(2)]
        s_t = [sb.tile([P, Q], F32, name="s_t%d" % j) for j in range(PACK)]
        for j in range(PACK):
            cols = slice(j * P, (j + 1) * P)
            nc.tensor.matmul_mx(out=a_t[j // 2][:, j % 2, :], lhsT=k_words[:, cols].bitcast(FP4X4), lhsT_scale=k_bytes[:, cols],
                                rhs=q_words[:].bitcast(FP8X4), rhs_scale=q_bytes[:], start=True, stop=True)
        for j in range(PACK):
            nc.scalar.activation(out=s_t[j][:], in_=a_t[j // 2][:, j % 2, :], func=ACT.Copy, scale=ks_col[:, j : j + 1])
        s = [bank(5 + h, [P, I], "s%d" % h) for h in range(HALVES)]
        for h in range(HALVES):
            for j in range(PACK):
                nc.tensor.transpose(s[h][:, j * P : (j + 1) * P], s_t[j][:, h * P : (h + 1) * P], ident[:])

        f_row = sb.tile([P, I], F32, name="f_row")
        nc.vector.tensor_tensor(f_row[:], vs_win[:].indirect(pages[:]), size_row[:], ALU.mult)

        v_bytes = sb.tile([P, PACK * P], U8, name="v_bytes", align_bytes=64)
        v_pairs = sb.tile([P, PACK * P, 2], F32, name="v_pairs", align_bytes=64)
        v_words = []

        def turn(rows, turned, pairs):
            words = rows[:].bitcast(F32)
            for u in range(2):
                nc.tensor.transpose(turned[:, u, :], words[:, u : I // 2 : 2], ident[:])
            nc.scalar.copy(out=pairs, in_=turned[:].rearrange("p u c -> p c u"))

        def gather_values(j, slot):
            v_bf = sb.tile([P, I], BF16, name="v_bf%d" % j, tag=slot, align_bytes=64)
            nc.vector.tensor_copy(v_bf[:], v_win[j][:].indirect(tokens[:]))
            return v_bf

        def turn_values(j, v_bf):
            turn(v_bf, bank((5, 7, 0, 7)[j], [P, 2, P], "v_t%d" % j), v_pairs[:, j * P : (j + 1) * P, :])

        def quantize(pairs, words, scale_bytes):
            nc.vector.quantize_mx(out=words.bitcast(FP8X4), scales=scale_bytes, in_=pairs.rearrange("p c u -> p (c u)").bitcast(BF16))

        def quantize_values(start, count, words):
            cols = slice(start * P, (start + count) * P)
            quantize(v_pairs[:, cols, :], words[:], v_bytes[:, cols])
            v_words.extend([words[:, n * P : (n + 1) * P] for n in range(count)])

        v_first = gather_values(0, "v_bf0")

        neg_max = [first.tile([P, 1], F32, name="neg_max%d" % h, offset=64 * h, align_bytes=64) for h in range(HALVES)]
        total = [sb.tile([P, 1], F32, name="total%d" % h) for h in range(HALVES)]
        p = [sb.tile([P, I], F32, name="p%d" % h, tag="p%d" % h, align_bytes=64) for h in range(HALVES)]
        for h in range(HALVES):
            nc.vector.tensor_reduce(out=neg_max[h][:], in_=s[h][:], axis=mybir.AxisListType.X, op=ALU.max, negate=True)
            nc.scalar.activation(out=p[h][:], in_=s[h][:], func=ACT.Exp, bias=neg_max[h][:], accum_out=total[h][:])

        turn_values(0, v_first)
        turn_values(1, gather_values(1, "v_bf1"))

        inv = [second.tile([P, 1], F32, name="inv%d" % h, offset=64 * h, align_bytes=64) for h in range(HALVES)]
        w_bytes = sb.tile([P, Q], U8, name="w_bytes", align_bytes=64)
        w_pairs = [sb.tile([P, P, 2], F32, name="w_pairs%d" % h, tag="w_pairs%d" % h, align_bytes=64) for h in range(HALVES)]
        for h in range(HALVES):
            nc.vector.reciprocal(out=inv[h][:], in_=total[h][:])
        for h in range(HALVES):
            w_bf = sb.tile([P, I], BF16, name="w_bf%d" % h, align_bytes=64)
            nc.vector.scalar_tensor_tensor(out=w_bf[:], in0=p[h][:], scalar=inv[h][:], in1=f_row[:], op0=ALU.mult, op1=ALU.mult)
            turn(w_bf, bank(5 + h, [P, 2, P], "w_t%d" % h), w_pairs[h][:])
        quantize_values(0, 2, sb.tile([P, 2 * P], U32, name="v_words01", tag="p0", align_bytes=64))

        turn_values(2, gather_values(2, "p1"))
        w_words = sb.tile([P, Q], U32, name="w_words", tag="v_win2", align_bytes=64)
        for h in range(HALVES):
            cols = slice(h * P, (h + 1) * P)
            quantize(w_pairs[h][:], w_words[:, cols], w_bytes[:, cols])
        v_last = gather_values(3, "w_pairs0")

        o = [[bank((3, 1)[g] + h, [P, 2, P], "o%d%d" % (g, h)) for h in range(HALVES)] for g in range(2)]
        o_bf = [last.tile([P, P, PACK], BF16, name="o_bf%d" % h, offset=1024 * (h + 1), align_bytes=64) for h in range(HALVES)]
        o_words = sb.tile([P, Q], U32, name="o_words", align_bytes=64)
        o_bytes = sb.tile([P, Q], U8, name="o_bytes", align_bytes=64)
        out_rows = out_0.rearrange("(p j) q -> p j q", j=PACK)

        def product(j):
            for h in reversed(range(HALVES)):
                cols = slice(h * P, (h + 1) * P)
                nc.tensor.matmul_mx(out=o[j // 2][h][:, j % 2, :], lhsT=v_words[j].bitcast(FP8X4), lhsT_scale=v_bytes[:, j * P : (j + 1) * P],
                                    rhs=w_words[:, cols].bitcast(FP8X4), rhs_scale=w_bytes[:, cols], start=True, stop=True)

        def rounded(g, h):
            return dict(out=o_bf[h][:, :, 2 * g : 2 * g + 2], in_=o[g][h][:].rearrange("p j q -> p q j"))

        def store(start, count, engine):
            o_sb = sb.tile([P, count, Q], F32, name="o_sb%d" % start)
            for h in reversed(range(HALVES)):
                nc.scalar.copy(out=o_sb[:, :, h * P : (h + 1) * P], in_=o[start // 2][h][:, start % 2 : start % 2 + count, :])
            engine.dma_start(out_rows[:, start : start + count, :], o_sb[:])

        quantize_values(2, 1, last.tile([P, P], U32, name="v_words2", offset=0, align_bytes=64))
        product(0)
        product(1)
        store(0, 2, nc.sync)
        turn_values(3, v_last)
        product(2)
        store(2, 1, nc.sync)
        for h in range(HALVES):
            nc.vector.tensor_copy(**rounded(0, h))
        quantize_values(3, 1, sb.tile([P, P], U32, name="v_words3", align_bytes=64))
        product(3)
        nc.vector.tensor_copy(**rounded(1, 0))
        nc.scalar.copy(**rounded(1, 1))
        for h in reversed(range(HALVES)):
            cols = slice(h * P, (h + 1) * P)
            nc.vector.quantize_mx(out=o_words[:, cols].bitcast(FP8X4), scales=o_bytes[:, cols], in_=o_bf[h][:].rearrange("p q j -> p (q j)"))
        store(3, 1, nc.scalar)
        nc.sync.dma_start(out_1[0].rearrange("p c r -> p (c r)").bitcast(I32), o_words[:].bitcast(I32))
        for quad in range(4):
            engine = nc.sync if quad < 2 else nc.scalar
            engine.dma_start(out_2[0, 4 * quad : 4 * quad + 4, :].bitcast(I32), o_bytes[32 * quad : 32 * quad + 4, :].bitcast(I32))
